import numpy as np
import ml_dtypes


def mxq(x, axis, fmt="e4m3"):
    dtype, down = {"e4m3": (ml_dtypes.float8_e4m3fn, 7), "e5m2": (ml_dtypes.float8_e5m2, 14)}[fmt]
    v = np.moveaxis(np.asarray(x, np.float32).astype(ml_dtypes.bfloat16).astype(np.float64), axis, -1)
    blocks = v.reshape(v.shape[:-1] + (-1, 32))
    amax = np.abs(blocks).max(-1, keepdims=True)
    byte = np.maximum(np.where(amax > 0, np.frexp(amax)[1] - 1 + 127, 0) - down, 1)
    scale = np.exp2(byte - 127.0)
    codes = (blocks / scale).astype(np.float32).astype(dtype).astype(np.float64)
    return np.moveaxis((codes * scale).reshape(v.shape), -1, axis)


WIDE = False


def mx_kscale(k):
    if not WIDE:
        return np.ones(k)
    levels = np.array([10, -10, 5, -5, 0])
    if k % 512:
        return np.exp2(np.random.permutation(np.resize(levels, k // 32))).repeat(32)
    a = np.empty((k // 512, 16))
    for p in range(k // 512):
        a[p, :8] = np.random.permutation(np.resize(levels, 8))
        for g in range(8):
            far = levels[np.abs(levels - a[p, g]) >= 10]
            a[p, g + 8] = far[np.random.randint(len(far))]
    return np.exp2(a.ravel()).repeat(32)


def f64(x):
    return np.asarray(x).astype(np.float64)


def striped(idx):
    return np.tile(np.asarray(idx).reshape(-1, 16).T, (8, 1)).astype(np.uint16)


def unstriped(offs):
    return offs[:16].T.reshape(-1).astype(np.int64)


E2M1 = np.array([0.0, 0.5, 1.0, 1.5, 2.0, 3.0, 4.0, 6.0, -0.0, -0.5, -1.0, -1.5, -2.0, -3.0, -4.0, -6.0])


def pack_weight(w, fmt):
    k, n = w.shape
    w = f64(np.asarray(w, np.float32).astype(ml_dtypes.bfloat16)).reshape(k // 32, 32, n)
    amax = np.abs(w).max(1)
    if fmt == "e4m3":
        byte = np.frexp(amax)[1] - 1 + 127 - 7
    else:
        mant, ex = np.frexp(amax / 6.0)
        byte = np.where(mant > 0.5, ex, ex - 1) + 127
    byte = np.clip(np.where(amax > 0, byte, 1), 1, 254)
    scaled = (w * np.exp2(127.0 - byte)[:, None, :]).reshape(k, n).astype(np.float32)
    by_word = np.ascontiguousarray(scaled.reshape(k // 512, 128, 4, n).transpose(0, 1, 3, 2))
    if fmt == "e4m3":
        words = by_word.astype(ml_dtypes.float8_e4m3fn).view(np.uint8)
    else:
        c = by_word.astype(ml_dtypes.float4_e2m1fn).view(np.uint8) & 0xF
        words = (c[..., 0::2] | (c[..., 1::2] << 4)).reshape(k // 512, 128, 2 * n)
    return np.ascontiguousarray(words), np.ascontiguousarray(byte.astype(np.uint8).reshape(k // 512, 16, n))


def unpack_weight(words, scales, fmt):
    g, _, n = scales.shape
    words = np.ascontiguousarray(words).reshape(g, 128, n, -1)
    if fmt == "e4m3":
        vals = words.view(ml_dtypes.float8_e4m3fn).astype(np.float64)
    else:
        nib = np.empty((g, 128, n, 4), np.uint8)
        nib[..., 0::2] = words & 0xF
        nib[..., 1::2] = words >> 4
        vals = E2M1[nib]
    vals = vals * np.repeat(np.exp2(scales.astype(np.float64) - 127.0), 8, axis=1)[..., None]
    return vals.transpose(0, 1, 3, 2).reshape(g * 512, n)


D, E, T, I, Q = 512, 512, 2048, 512, 128


def setup_inputs():
    n = np.random.standard_normal
    idx = np.random.permutation(T)[:I]
    fd = mx_kscale(D)
    fe = mx_kscale(E)
    keysp = pack_weight(n((D, T)) / fd[:, None], "e2m1")
    valsp = pack_weight(n((E, T)) / fe[:, None], "e2m1")
    return {
        "query": (n((D, Q)) * 0.7 / np.sqrt(D) * fd[:, None]).astype(np.float32),
        "keys_words": keysp[0],
        "keys_scales": keysp[1],
        "gout": (n((E, Q)) * 1 / np.sqrt(E) * fe[:, None]).astype(np.float32),
        "vals_words": valsp[0],
        "vals_scales": valsp[1],
        "base": (0.5 * n((Q, I))).astype(np.float32),
        "offs": striped(idx),
    }


def reference(query, keys_words, keys_scales, gout, vals_words, vals_scales, base, offs):
    idx = unstriped(offs)
    keysu = unpack_weight(keys_words, keys_scales, "e2m1")
    valsu = unpack_weight(vals_words, vals_scales, "e2m1")
    queryq = mxq(f64(query), 0, "e4m3")
    keysidxg = keysu[:, idx]
    a = queryq.T @ keysidxg
    p = np.exp(a - np.max(a, axis=1, keepdims=True))
    n2 = np.sqrt(np.sum(np.square(p), axis=1, keepdims=True))
    goutq = mxq(f64(gout), 0, "e4m3")
    valsidxg = valsu[:, idx]
    c0 = goutq.T @ valsidxg
    dn2 = np.sum(c0 * p / np.square(n2) * (-1.0), axis=1, keepdims=True)
    dp = c0 / n2 + dn2 * 0.5 / np.sqrt(np.sum(np.square(p), axis=1, keepdims=True)) * p * 2.0
    da = dp * p
    hda = da * 16.0 * 2.0 * 16.0
    hdp = hda * p
    hdn2 = np.sum(hdp * 2.0 * p, axis=1, keepdims=True) / np.sqrt(np.sum(np.square(p), axis=1, keepdims=True)) * 0.5
    hn2 = np.sum(hdp * c0 / np.square(n2) * (-1.0), axis=1, keepdims=True) + np.sum(hdn2 * (-1.0) * c0 * p / np.square(np.square(n2)) * (-1.0), axis=1, keepdims=True) * n2 * 2.0
    hp = hda * dp + np.sum(hdp * 2.0 * p, axis=1, keepdims=True) * dn2 * 0.5 / np.square(np.sqrt(np.sum(np.square(p), axis=1, keepdims=True))) * (-1.0) * 0.5 / np.sqrt(np.sum(np.square(p), axis=1, keepdims=True)) * p * 2.0 + hdp * 2.0 * dn2 * 0.5 / np.sqrt(np.sum(np.square(p), axis=1, keepdims=True)) + hdn2 * (-1.0) / np.square(n2) * c0 + hn2 * 0.5 / np.sqrt(np.sum(np.square(p), axis=1, keepdims=True)) * p * 2.0
    ha = hp * p
    y = ha + f64(base)
    return y

@@ -1,0 +1,147 @@
+import math
+from contextlib import ExitStack
+
+import concourse.mybir as mybir
+
+D, E, T, I, Q = 512, 512, 2048, 512, 128
+FLOPS = 2 * Q * I * (D + E)
+
+F32 = mybir.dt.float32
+BF16 = mybir.dt.bfloat16
+I32 = mybir.dt.int32
+U32 = mybir.dt.uint32
+U16 = mybir.dt.uint16
+U8 = mybir.dt.uint8
+FP8X4 = mybir.dt.float8_e4m3fn_x4
+FP4X4 = mybir.dt.float4_e2m1fn_x4
+ALU = mybir.AluOpType
+ACT = mybir.ActivationFunctionType
+AX = mybir.AxisListType
+
+P = 128
+PACK = 4
+PENALTY = 16.0 * 2.0 * 16.0
+
+
+def tile_attend_gpunitweights_kernel(tc, query, keys_words, keys_scales, gout, vals_words, vals_scales, base, offs, out):
+    nc = tc.nc
+    with ExitStack() as ctx:
+        sb = ctx.enter_context(tc.tile_pool(name="sb", bufs=1))
+        ps = ctx.enter_context(tc.psum_pool(name="ps", bufs=1))
+
+        def col(name, width=1):
+            return sb.tile([P, width], F32, name=name)
+
+        def row(name):
+            return sb.tile([P, I], F32, name=name)
+
+        offsets = sb.tile([P, I // 16], U16, name="offsets")
+        nc.sync.dma_start(offsets[:], offs)
+
+        k_pool = sb.tile([P, T], U16, name="k_pool", align_bytes=64)
+        v_pool = sb.tile([P, T], U16, name="v_pool", align_bytes=64)
+        ks_pool = sb.tile([P, T], U8, name="ks_pool", align_bytes=64)
+        vs_pool = sb.tile([P, T], U8, name="vs_pool", align_bytes=64)
+        q_raw = sb.tile([P, PACK, Q], F32, name="q_raw")
+        g_raw = sb.tile([P, PACK, Q], F32, name="g_raw")
+        base_sb = row("base_sb")
+
+        nc.scalar.dma_start(k_pool[:].bitcast(I32), keys_words[0].bitcast(I32))
+        nc.scalar.dma_start(q_raw[:], query.rearrange("(p j) q -> p j q", j=PACK))
+
+        warm_in = col("warm_in")
+        warm_out = col("warm_out")
+        nc.gpsimd.memset(warm_in[:], 0.0)
+        nc.scalar.activation(warm_out[:], warm_in[:], ACT.Exp)
+
+        for pool, scales in ((ks_pool, keys_scales), (vs_pool, vals_scales)):
+            nc.vector.memset(pool[:].bitcast(I32), 0)
+            rows = scales[0].rearrange("(g r) t -> r g t", r=4)
+            for r in range(4):
+                nc.sync.dma_start(pool[r:P:32, :].bitcast(I32), rows[r].bitcast(I32))
+
+        nc.scalar.dma_start(g_raw[:], gout.rearrange("(p j) q -> p j q", j=PACK))
+        nc.scalar.dma_start(v_pool[:].bitcast(I32), vals_words[0].bitcast(I32))
+        nc.sync.dma_start(base_sb[:], base)
+
+        factors = col("factors", 3)
+        for j, value in enumerate((-1.0, 1.5, 0.5)):
+            nc.gpsimd.memset(factors[:, j : j + 1], value)
+
+        def gather(name, pool, dtype):
+            picked = sb.tile([P, I], dtype, name=name, align_bytes=64)
+            nc.vector.tensor_copy(picked[:], pool[:].indirect(offsets[:]))
+            return picked
+
+        def cast(name, raw):
+            grouped = sb.tile([P, Q, PACK], BF16, name=name, align_bytes=64)
+            nc.scalar.copy(grouped[:], raw[:].rearrange("p j q -> p q j"))
+            return grouped
+
+        def quantize(name, grouped):
+            codes = sb.tile([P, Q], U32, name=name + "_codes", align_bytes=64)
+            scales = sb.tile([P, Q], U8, name=name + "_scales", align_bytes=64)
+            nc.vector.quantize_mx(out=codes[:].bitcast(FP8X4), scales=scales[:], in_=grouped[:].rearrange("p q j -> p (q j)"))
+            return codes, scales
+
+        def product(name, rows, words, scales):
+            acc = ps.tile([P, I], F32, name=name)
+            nc.tensor.matmul_mx(out=acc[:], lhsT=rows[0][:].bitcast(FP8X4), lhsT_scale=rows[1][:],
+                                rhs=words[:].bitcast(FP4X4), rhs_scale=scales[:], start=True, stop=True)
+            return acc
+
+        q_bf = cast("q_bf", q_raw)
+        k_words = gather("k_words", k_pool, U16)
+        k_scales = gather("k_scales", ks_pool, U8)
+        q_mx = quantize("q", q_bf)
+        a = product("a", q_mx, k_words, k_scales)
+        g_bf = cast("g_bf", g_raw)
+        v_scales = gather("v_scales", vs_pool, U8)
+
+        neg_max = col("neg_max")
+        nc.vector.tensor_reduce(neg_max[:], a[:], AX.X, ALU.max, negate=True)
+        g_mx = quantize("g", g_bf)
+        v_words = gather("v_words", v_pool, U16)
+        c = product("c", g_mx, v_words, v_scales)
+
+        p, q, qq = row("p"), row("q"), row("qq")
+        s2, q2 = col("s2"), col("q2")
+        nc.scalar.activation(p[:], a[:], ACT.Exp, bias=neg_max[:])
+        nc.scalar.activation(q[:], p[:], ACT.Square, accum_out=s2[:])
+        nc.scalar.activation(qq[:], q[:], ACT.Square, accum_out=q2[:])
+
+        r = col("r")
+        rv = col("rv", 4)
+        nq = col("nq", 2)
+        nc.vector.reciprocal(r[:], s2[:])
+        nc.vector.tensor_scalar(rv[:, 0:3], factors[:], r[:], None, ALU.mult)
+        nc.vector.tensor_scalar(rv[:, 3:4], r[:], r[:], 5.0, ALU.mult, ALU.mult)
+
+        u, uq, uu = row("u"), row("uq"), row("uu")
+        c1, uqh, u2r = col("c1"), col("uqh"), col("u2r")
+        nc.vector.scalar_tensor_tensor(u[:], c[:], math.sqrt(PENALTY), p[:], ALU.mult, ALU.mult, accum_out=c1[:])
+        nc.vector.tensor_scalar(nq[:, 0:1], q2[:], r[:], -1.0 / 3.0, ALU.mult, ALU.mult)
+        nc.vector.tensor_scalar(nq[:, 1:2], q2[:], r[:], -1.0 / 5.0, ALU.mult, ALU.mult)
+        mv = col("mv", 3)
+        nc.vector.tensor_scalar(mv[:], rv[:, 1:4], c1[:], None, ALU.mult)
+        nc.vector.scalar_tensor_tensor(uq[:], u[:], rv[:, 2:3], q[:], ALU.mult, ALU.mult, accum_out=uqh[:])
+        nc.scalar.activation(uu[:], u[:], ACT.Square, scale=r[:], accum_out=u2r[:])
+
+        k3, bt, nb, k5 = col("k3"), col("bt", 2), col("nb"), col("k5")
+        vn, b1, y, f1, x, res = row("vn"), row("b1"), row("y"), row("f1"), row("x"), row("res")
+        nc.vector.tensor_scalar(k3[:], mv[:, 1:2], mv[:, 1:2], rv[:, 0:1], ALU.mult, ALU.mult)
+        H = I // 2
+        lo, hi = slice(0, H), slice(H, I)
+        nc.vector.scalar_tensor_tensor(vn[:, lo], q[:, lo], mv[:, 0:1], u[:, lo], ALU.mult, ALU.subtract)
+        nc.vector.tensor_scalar(bt[:], nq[:], mv[:, 0:1], uqh[:], ALU.mult, ALU.add)
+        nc.vector.scalar_tensor_tensor(vn[:, hi], q[:, hi], mv[:, 0:1], u[:, hi], ALU.mult, ALU.subtract)
+        nc.vector.tensor_scalar(nb[:], bt[:, 0:1], bt[:, 0:1], rv[:, 0:1], ALU.mult, ALU.mult)
+        nc.vector.tensor_scalar(k5[:], bt[:, 1:2], mv[:, 2:3], u2r[:], ALU.mult, ALU.subtract)
+        nc.vector.scalar_tensor_tensor(b1[:], qq[:], k3[:], base_sb[:], ALU.mult, ALU.add)
+        nc.scalar.activation(y[:], q[:], ACT.Identity, scale=k5[:], bias=nb[:])
+        nc.scalar.activation(f1[:], vn[:], ACT.Square, bias=bt[:, 0:1])
+        for half in (lo, hi):
+            nc.vector.tensor_tensor(x[:, half], b1[:, half], y[:, half], ALU.add)
+        for half, queue in ((lo, nc.sync), (hi, nc.scalar)):
+            nc.vector.scalar_tensor_tensor(res[:, half], f1[:, half], r[:], x[:, half], ALU.mult, ALU.add)
+            queue.dma_start(out[:, half], res[:, half])

@@ -27,6 +27,7 @@ def tile_attend_gpunitweights_kernel(tc, query, keys_words, keys_scales, gout, v
     nc = tc.nc
     with ExitStack() as ctx:
         sb = ctx.enter_context(tc.tile_pool(name="sb", bufs=1))
+        reuse = ctx.enter_context(tc.tile_pool(name="reuse", bufs=1))
         ps = ctx.enter_context(tc.psum_pool(name="ps", bufs=1))
 
         def col(name, width=1):
@@ -39,20 +40,12 @@ def tile_attend_gpunitweights_kernel(tc, query, keys_words, keys_scales, gout, v
         nc.sync.dma_start(offsets[:], offs)
 
         k_pool = sb.tile([P, T], U16, name="k_pool", align_bytes=64)
-        v_pool = sb.tile([P, T], U16, name="v_pool", align_bytes=64)
         ks_pool = sb.tile([P, T], U8, name="ks_pool", align_bytes=64)
-        vs_pool = sb.tile([P, T], U8, name="vs_pool", align_bytes=64)
-        q_raw = sb.tile([P, PACK, Q], F32, name="q_raw")
-        g_raw = sb.tile([P, PACK, Q], F32, name="g_raw")
-        base_sb = row("base_sb")
+        vs_pool = reuse.tile([P, T], U8, name="vs_pool", offset=0, align_bytes=64)
+        q_raw = sb.tile([P, PACK, Q], F32, name="q_raw", tag="words", align_bytes=64)
 
-        nc.scalar.dma_start(k_pool[:].bitcast(I32), keys_words[0].bitcast(I32))
-        nc.scalar.dma_start(q_raw[:], query.rearrange("(p j) q -> p j q", j=PACK))
-
-        warm_in = col("warm_in")
-        warm_out = col("warm_out")
-        nc.gpsimd.memset(warm_in[:], 0.0)
-        nc.scalar.activation(warm_out[:], warm_in[:], ACT.Exp)
+        nc.sync.dma_start(k_pool[:].bitcast(I32), keys_words[0].bitcast(I32))
+        nc.sync.dma_start(q_raw[:], query.rearrange("(p j) q -> p j q", j=PACK))
 
         for pool, scales in ((ks_pool, keys_scales), (vs_pool, vals_scales)):
             nc.vector.memset(pool[:].bitcast(I32), 0)
@@ -60,16 +53,24 @@ def tile_attend_gpunitweights_kernel(tc, query, keys_words, keys_scales, gout, v
             for r in range(4):
                 nc.sync.dma_start(pool[r:P:32, :].bitcast(I32), rows[r].bitcast(I32))
 
+
+        warm_in = col("warm_in")
+        warm_out = sb.tile([P, 1], F32, name="warm_out", tag="stage")
+        nc.vector.memset(warm_in[:], 0.0)
+        nc.scalar.activation(warm_out[:], warm_in[:], ACT.Exp)
+        g_raw = sb.tile([P, PACK, Q], F32, name="g_raw", tag="stage")
         nc.scalar.dma_start(g_raw[:], gout.rearrange("(p j) q -> p j q", j=PACK))
-        nc.scalar.dma_start(v_pool[:].bitcast(I32), vals_words[0].bitcast(I32))
-        nc.sync.dma_start(base_sb[:], base)
 
         factors = col("factors", 3)
         for j, value in enumerate((-1.0, 1.5, 0.5)):
             nc.gpsimd.memset(factors[:, j : j + 1], value)
 
-        def gather(name, pool, dtype):
-            picked = sb.tile([P, I], dtype, name=name, align_bytes=64)
+        powers = col("powers", 2)
+        for j, value in enumerate((0.5, 2.0)):
+            nc.gpsimd.memset(powers[:, j : j + 1], value)
+
+        def gather(name, pool, dtype, tag):
+            picked = sb.tile([P, I], dtype, name=name, tag=tag, align_bytes=64)
             nc.vector.tensor_copy(picked[:], pool[:].indirect(offsets[:]))
             return picked
 
@@ -78,70 +79,86 @@ def tile_attend_gpunitweights_kernel(tc, query, keys_words, keys_scales, gout, v
             nc.scalar.copy(grouped[:], raw[:].rearrange("p j q -> p q j"))
             return grouped
 
-        def quantize(name, grouped):
-            codes = sb.tile([P, Q], U32, name=name + "_codes", align_bytes=64)
+        def quantize(name, grouped, codes):
             scales = sb.tile([P, Q], U8, name=name + "_scales", align_bytes=64)
             nc.vector.quantize_mx(out=codes[:].bitcast(FP8X4), scales=scales[:], in_=grouped[:].rearrange("p q j -> p (q j)"))
             return codes, scales
 
         def product(name, rows, words, scales):
-            acc = ps.tile([P, I], F32, name=name)
+            acc = ps.tile([P, words.shape[1]], F32, name=name)
             nc.tensor.matmul_mx(out=acc[:], lhsT=rows[0][:].bitcast(FP8X4), lhsT_scale=rows[1][:],
-                                rhs=words[:].bitcast(FP4X4), rhs_scale=scales[:], start=True, stop=True)
+                                rhs=words.bitcast(FP4X4), rhs_scale=scales, start=True, stop=True)
             return acc
 
         q_bf = cast("q_bf", q_raw)
-        k_words = gather("k_words", k_pool, U16)
-        k_scales = gather("k_scales", ks_pool, U8)
-        q_mx = quantize("q", q_bf)
-        a = product("a", q_mx, k_words, k_scales)
+        k_words = gather("k_words", k_pool, U16, "picked")
+        v_pool = sb.tile([P, T], U16, name="v_pool", tag="words", align_bytes=64)
+        nc.sync.dma_start(v_pool[:].bitcast(I32), vals_words[0].bitcast(I32))
+        k_scales = gather("k_scales", ks_pool, U8, "k_scales")
+        q_mx = quantize("q", q_bf, sb.tile([P, Q], U32, name="q_codes", align_bytes=64))
+        a = product("a", q_mx, k_words[:], k_scales[:])
         g_bf = cast("g_bf", g_raw)
-        v_scales = gather("v_scales", vs_pool, U8)
+        base_sb = sb.tile([P, I], F32, name="base_sb", tag="stage")
+        nc.sync.dma_start(base_sb[:], base)
+        v_scales = gather("v_scales", vs_pool, U8, "v_scales")
 
-        neg_max = col("neg_max")
-        nc.vector.tensor_reduce(neg_max[:], a[:], AX.X, ALU.max, negate=True)
-        g_mx = quantize("g", g_bf)
-        v_words = gather("v_words", v_pool, U16)
-        c = product("c", g_mx, v_words, v_scales)
+        neg_max = reuse.tile([P, 1], F32, name="neg_max", offset=1024, align_bytes=64)
+        g_mx = quantize("g", g_bf, reuse.tile([P, Q], U32, name="g_codes", offset=0, align_bytes=64))
+        scratch = row("scratch")
+        nc.vector.tensor_scalar(scratch[:], a[:], -2.0, None, ALU.mult, ALU.min, accum_out=neg_max[:])
+        H = I // 2
+        lo, hi = slice(0, H), slice(H, I)
+        v_words = sb.tile([P, I], U16, name="v_words", tag="picked", align_bytes=64)
+        c = []
+        for h, half in enumerate((lo, hi)):
+            nc.vector.tensor_copy(v_words[:, half], v_pool[:].indirect(offsets[:, h * (H // 16) : (h + 1) * (H // 16)]))
+            c.append(product("c%d" % h, g_mx, v_words[:, half], v_scales[:, half]))
 
         p, q, qq = row("p"), row("q"), row("qq")
         s2, q2 = col("s2"), col("q2")
-        nc.scalar.activation(p[:], a[:], ACT.Exp, bias=neg_max[:])
-        nc.scalar.activation(q[:], p[:], ACT.Square, accum_out=s2[:])
-        nc.scalar.activation(qq[:], q[:], ACT.Square, accum_out=q2[:])
+        shifts = col("shifts", 2)
+        nc.scalar.activation(shifts[:], powers[:], ACT.Copy, scale=neg_max[:])
+        nc.scalar.activation(q[:], a[:], ACT.Exp, scale=2.0, bias=neg_max[:], accum_out=s2[:])
+        nc.scalar.activation(p[:], a[:], ACT.Exp, bias=shifts[:, 0:1])
+        nc.scalar.activation(qq[:], a[:], ACT.Exp, scale=4.0, bias=shifts[:, 1:2], accum_out=q2[:])
 
-        r = col("r")
+        r = sb.tile([P, 1], F32, name="r", tag="words", align_bytes=64)
         rv = col("rv", 4)
-        nq = col("nq", 2)
+        nq = sb.tile([P, 2], F32, name="nq", tag="picked", align_bytes=64)
         nc.vector.reciprocal(r[:], s2[:])
         nc.vector.tensor_scalar(rv[:, 0:3], factors[:], r[:], None, ALU.mult)
         nc.vector.tensor_scalar(rv[:, 3:4], r[:], r[:], 5.0, ALU.mult, ALU.mult)
 
         u, uq, uu = row("u"), row("uq"), row("uu")
-        c1, uqh, u2r = col("c1"), col("uqh"), col("u2r")
-        nc.vector.scalar_tensor_tensor(u[:], c[:], math.sqrt(PENALTY), p[:], ALU.mult, ALU.mult, accum_out=c1[:])
+        c_lo, c_hi, uq_lo, uq_hi, u2r = col("c_lo"), col("c_hi"), col("uq_lo"), col("uq_hi"), col("u2r")
+        mv_lo, mv = col("mv_lo", 3), col("mv", 3)
+        k3, bt_lo, bt, nb, k5 = col("k3"), col("bt_lo", 2), col("bt", 2), col("nb"), col("k5")
+        vn, b1, y, f1, x, res = row("vn"), row("b1"), row("y"), row("f1"), row("x"), row("res")
+        root = math.sqrt(PENALTY)
+        nc.vector.scalar_tensor_tensor(u[:, lo], c[0][:], root, p[:, lo], ALU.mult, ALU.mult, accum_out=c_lo[:])
+        nc.vector.tensor_scalar(mv_lo[:], rv[:, 1:4], c_lo[:], None, ALU.mult)
+        nc.vector.scalar_tensor_tensor(u[:, hi], c[1][:], root, p[:, hi], ALU.mult, ALU.mult, accum_out=c_hi[:])
+        nc.vector.scalar_tensor_tensor(uq[:, lo], u[:, lo], rv[:, 2:3], q[:, lo], ALU.mult, ALU.mult, accum_out=uq_lo[:])
+        nc.vector.scalar_tensor_tensor(mv[:], rv[:, 1:4], c_hi[:], mv_lo[:], ALU.mult, ALU.add)
         nc.vector.tensor_scalar(nq[:, 0:1], q2[:], r[:], -1.0 / 3.0, ALU.mult, ALU.mult)
         nc.vector.tensor_scalar(nq[:, 1:2], q2[:], r[:], -1.0 / 5.0, ALU.mult, ALU.mult)
-        mv = col("mv", 3)
-        nc.vector.tensor_scalar(mv[:], rv[:, 1:4], c1[:], None, ALU.mult)
-        nc.vector.scalar_tensor_tensor(uq[:], u[:], rv[:, 2:3], q[:], ALU.mult, ALU.mult, accum_out=uqh[:])
+        nc.vector.scalar_tensor_tensor(uq[:, hi], u[:, hi], rv[:, 2:3], q[:, hi], ALU.mult, ALU.mult, accum_out=uq_hi[:])
         nc.scalar.activation(uu[:], u[:], ACT.Square, scale=r[:], accum_out=u2r[:])
-
-        k3, bt, nb, k5 = col("k3"), col("bt", 2), col("nb"), col("k5")
-        vn, b1, y, f1, x, res = row("vn"), row("b1"), row("y"), row("f1"), row("x"), row("res")
+        nc.vector.tensor_scalar(bt_lo[:], nq[:], mv[:, 0:1], uq_lo[:], ALU.mult, ALU.add)
         nc.vector.tensor_scalar(k3[:], mv[:, 1:2], mv[:, 1:2], rv[:, 0:1], ALU.mult, ALU.mult)
-        H = I // 2
-        lo, hi = slice(0, H), slice(H, I)
         nc.vector.scalar_tensor_tensor(vn[:, lo], q[:, lo], mv[:, 0:1], u[:, lo], ALU.mult, ALU.subtract)
-        nc.vector.tensor_scalar(bt[:], nq[:], mv[:, 0:1], uqh[:], ALU.mult, ALU.add)
+        nc.vector.tensor_scalar(bt[:], bt_lo[:], uq_hi[:], None, ALU.add)
         nc.vector.scalar_tensor_tensor(vn[:, hi], q[:, hi], mv[:, 0:1], u[:, hi], ALU.mult, ALU.subtract)
         nc.vector.tensor_scalar(nb[:], bt[:, 0:1], bt[:, 0:1], rv[:, 0:1], ALU.mult, ALU.mult)
         nc.vector.tensor_scalar(k5[:], bt[:, 1:2], mv[:, 2:3], u2r[:], ALU.mult, ALU.subtract)
-        nc.vector.scalar_tensor_tensor(b1[:], qq[:], k3[:], base_sb[:], ALU.mult, ALU.add)
-        nc.scalar.activation(y[:], q[:], ACT.Identity, scale=k5[:], bias=nb[:])
-        nc.scalar.activation(f1[:], vn[:], ACT.Square, bias=bt[:, 0:1])
         for half in (lo, hi):
-            nc.vector.tensor_tensor(x[:, half], b1[:, half], y[:, half], ALU.add)
+            nc.vector.scalar_tensor_tensor(b1[:, half], qq[:, half], k3[:], base_sb[:, half], ALU.mult, ALU.add)
+        for half in (lo, hi):
+            nc.scalar.activation(f1[:, half], vn[:, half], ACT.Square, bias=bt[:, 0:1])
+        for half in (lo, hi):
+            nc.scalar.activation(y[:, half], q[:, half], ACT.Identity, scale=k5[:], bias=nb[:])
+        for half in (lo, hi):
+            nc.vector.scalar_tensor_tensor(x[:, half], f1[:, half], r[:], b1[:, half], ALU.mult, ALU.add)
         for half, queue in ((lo, nc.sync), (hi, nc.scalar)):
-            nc.vector.scalar_tensor_tensor(res[:, half], f1[:, half], r[:], x[:, half], ALU.mult, ALU.add)
+            nc.vector.tensor_tensor(res[:, half], x[:, half], y[:, half], ALU.add)
             queue.dma_start(out[:, half], res[:, half])

@@ -16,18 +16,24 @@ FP8X4 = mybir.dt.float8_e4m3fn_x4
 FP4X4 = mybir.dt.float4_e2m1fn_x4
 ALU = mybir.AluOpType
 ACT = mybir.ActivationFunctionType
-AX = mybir.AxisListType
 
 P = 128
 PACK = 4
+QUADRANT = 32
+SCALE_ROWS = 4
+LIST_ROWS = 16
 PENALTY = 16.0 * 2.0 * 16.0
+HALF = I // 2
+HALVES = (slice(0, HALF), slice(HALF, I))
+MX_ALIGN = 64
 
 
 def tile_attend_gpunitweights_kernel(tc, query, keys_words, keys_scales, gout, vals_words, vals_scales, base, offs, out):
     nc = tc.nc
+    lo, hi = HALVES
     with ExitStack() as ctx:
         sb = ctx.enter_context(tc.tile_pool(name="sb", bufs=1))
-        reuse = ctx.enter_context(tc.tile_pool(name="reuse", bufs=1))
+        placed = ctx.enter_context(tc.tile_pool(name="placed", bufs=1))
         ps = ctx.enter_context(tc.psum_pool(name="ps", bufs=1))
 
         def col(name, width=1):
@@ -36,129 +42,147 @@ def tile_attend_gpunitweights_kernel(tc, query, keys_words, keys_scales, gout, v
         def row(name):
             return sb.tile([P, I], F32, name=name)
 
-        offsets = sb.tile([P, I // 16], U16, name="offsets")
-        nc.sync.dma_start(offsets[:], offs)
-
-        k_pool = sb.tile([P, T], U16, name="k_pool", align_bytes=64)
-        ks_pool = sb.tile([P, T], U8, name="ks_pool", align_bytes=64)
-        vs_pool = reuse.tile([P, T], U8, name="vs_pool", offset=0, align_bytes=64)
-        q_raw = sb.tile([P, PACK, Q], F32, name="q_raw", tag="words", align_bytes=64)
-
-        nc.sync.dma_start(k_pool[:].bitcast(I32), keys_words[0].bitcast(I32))
-        nc.sync.dma_start(q_raw[:], query.rearrange("(p j) q -> p j q", j=PACK))
-
-        for pool, scales in ((ks_pool, keys_scales), (vs_pool, vals_scales)):
-            nc.vector.memset(pool[:].bitcast(I32), 0)
-            rows = scales[0].rearrange("(g r) t -> r g t", r=4)
-            for r in range(4):
-                nc.sync.dma_start(pool[r:P:32, :].bitcast(I32), rows[r].bitcast(I32))
-
-
-        warm_in = col("warm_in")
-        warm_out = sb.tile([P, 1], F32, name="warm_out", tag="stage")
-        nc.vector.memset(warm_in[:], 0.0)
-        nc.scalar.activation(warm_out[:], warm_in[:], ACT.Exp)
-        g_raw = sb.tile([P, PACK, Q], F32, name="g_raw", tag="stage")
-        nc.scalar.dma_start(g_raw[:], gout.rearrange("(p j) q -> p j q", j=PACK))
-
-        factors = col("factors", 3)
-        for j, value in enumerate((-1.0, 1.5, 0.5)):
-            nc.gpsimd.memset(factors[:, j : j + 1], value)
-
-        powers = col("powers", 2)
-        for j, value in enumerate((0.5, 2.0)):
-            nc.gpsimd.memset(powers[:, j : j + 1], value)
-
         def gather(name, pool, dtype, tag):
-            picked = sb.tile([P, I], dtype, name=name, tag=tag, align_bytes=64)
+            picked = sb.tile([P, I], dtype, name=name, tag=tag, align_bytes=MX_ALIGN)
             nc.vector.tensor_copy(picked[:], pool[:].indirect(offsets[:]))
             return picked
 
-        def cast(name, raw):
-            grouped = sb.tile([P, Q, PACK], BF16, name=name, align_bytes=64)
-            nc.scalar.copy(grouped[:], raw[:].rearrange("p j q -> p q j"))
+        def interleave(name, raw):
+            grouped = sb.tile([P, Q, PACK], BF16, name=name, align_bytes=MX_ALIGN)
+            nc.scalar.copy(grouped[:], raw[:].rearrange("p t q -> p q t"))
             return grouped
 
         def quantize(name, grouped, codes):
-            scales = sb.tile([P, Q], U8, name=name + "_scales", align_bytes=64)
-            nc.vector.quantize_mx(out=codes[:].bitcast(FP8X4), scales=scales[:], in_=grouped[:].rearrange("p q j -> p (q j)"))
+            scales = sb.tile([P, Q], U8, name=name, align_bytes=MX_ALIGN)
+            nc.vector.quantize_mx(
+                out=codes[:].bitcast(FP8X4), scales=scales[:], in_=grouped[:].rearrange("p q t -> p (q t)")
+            )
             return codes, scales
 
         def product(name, rows, words, scales):
             acc = ps.tile([P, words.shape[1]], F32, name=name)
-            nc.tensor.matmul_mx(out=acc[:], lhsT=rows[0][:].bitcast(FP8X4), lhsT_scale=rows[1][:],
-                                rhs=words.bitcast(FP4X4), rhs_scale=scales, start=True, stop=True)
+            nc.tensor.matmul_mx(
+                out=acc[:],
+                lhsT=rows[0][:].bitcast(FP8X4),
+                lhsT_scale=rows[1][:],
+                rhs=words.bitcast(FP4X4),
+                rhs_scale=scales,
+                start=True,
+                stop=True,
+            )
             return acc
 
-        q_bf = cast("q_bf", q_raw)
-        k_words = gather("k_words", k_pool, U16, "picked")
-        v_pool = sb.tile([P, T], U16, name="v_pool", tag="words", align_bytes=64)
-        nc.sync.dma_start(v_pool[:].bitcast(I32), vals_words[0].bitcast(I32))
-        k_scales = gather("k_scales", ks_pool, U8, "k_scales")
-        q_mx = quantize("q", q_bf, sb.tile([P, Q], U32, name="q_codes", align_bytes=64))
-        a = product("a", q_mx, k_words[:], k_scales[:])
-        g_bf = cast("g_bf", g_raw)
-        base_sb = sb.tile([P, I], F32, name="base_sb", tag="stage")
-        nc.sync.dma_start(base_sb[:], base)
-        v_scales = gather("v_scales", vs_pool, U8, "v_scales")
+        offsets = sb.tile([P, I // LIST_ROWS], U16, name="offsets")
+        key_pool = sb.tile([P, T], U16, name="key_pool", align_bytes=MX_ALIGN)
+        key_scale_pool = sb.tile([P, T], U8, name="key_scale_pool", align_bytes=MX_ALIGN)
+        val_scale_pool = placed.tile([P, T], U8, name="val_scale_pool", offset=0, align_bytes=MX_ALIGN)
+        query_raw = sb.tile([P, PACK, Q], F32, name="query_raw", tag="chain_a", align_bytes=MX_ALIGN)
 
-        neg_max = reuse.tile([P, 1], F32, name="neg_max", offset=1024, align_bytes=64)
-        g_mx = quantize("g", g_bf, reuse.tile([P, Q], U32, name="g_codes", offset=0, align_bytes=64))
-        scratch = row("scratch")
-        nc.vector.tensor_scalar(scratch[:], a[:], -2.0, None, ALU.mult, ALU.min, accum_out=neg_max[:])
-        H = I // 2
-        lo, hi = slice(0, H), slice(H, I)
-        v_words = sb.tile([P, I], U16, name="v_words", tag="picked", align_bytes=64)
-        c = []
-        for h, half in enumerate((lo, hi)):
-            nc.vector.tensor_copy(v_words[:, half], v_pool[:].indirect(offsets[:, h * (H // 16) : (h + 1) * (H // 16)]))
-            c.append(product("c%d" % h, g_mx, v_words[:, half], v_scales[:, half]))
+        nc.sync.dma_start(key_pool[:].bitcast(I32), keys_words[0].bitcast(I32))
+        nc.sync.dma_start(offsets[:], offs)
+        nc.sync.dma_start(query_raw[:], query.rearrange("(p t) q -> p t q", t=PACK))
+
+        for pool, scales in ((key_scale_pool, keys_scales), (val_scale_pool, vals_scales)):
+            nc.vector.memset(pool[:].bitcast(I32), 0)
+            by_place = scales[0].rearrange("(g j) t -> j g t", j=SCALE_ROWS)
+            for j in range(SCALE_ROWS):
+                nc.sync.dma_start(pool[j:P:QUADRANT, :].bitcast(I32), by_place[j].bitcast(I32))
+
+        zero = sb.tile([P, 1], F32, name="zero", tag="chain_b")
+        one = col("one")
+        fractions = col("fractions", 2)
+        nc.vector.memset(zero[:], 0.0)
+        nc.scalar.activation(one[:], zero[:], ACT.Exp)
+        for j, value in enumerate((-1.0 / 3.0, -1.0 / 5.0)):
+            nc.gpsimd.tensor_scalar(fractions[:, j : j + 1], one[:], value, 0.0, ALU.mult, ALU.add)
+        gout_raw = sb.tile([P, PACK, Q], F32, name="gout_raw", tag="chain_b")
+        nc.scalar.dma_start(gout_raw[:], gout.rearrange("(p t) q -> p t q", t=PACK))
+        r_factors = col("r_factors", 3)
+        for j, value in enumerate((-1.0, 1.5, 0.5)):
+            nc.gpsimd.memset(r_factors[:, j : j + 1], value)
+        max_factors = col("max_factors", 2)
+        for j, value in enumerate((0.5, 2.0)):
+            nc.gpsimd.memset(max_factors[:, j : j + 1], value)
+
+        query_bf = interleave("query_bf", query_raw)
+        key_words = gather("key_words", key_pool, U16, "chain_c")
+        val_pool = sb.tile([P, T], U16, name="val_pool", tag="chain_a", align_bytes=MX_ALIGN)
+        nc.sync.dma_start(val_pool[:].bitcast(I32), vals_words[0].bitcast(I32))
+        key_scales = gather("key_scales", key_scale_pool, U8, "key_scales")
+        query_codes = sb.tile([P, Q], U32, name="query_codes", align_bytes=MX_ALIGN)
+        query_mx = quantize("query_scales", query_bf, query_codes)
+        a = product("a", query_mx, key_words[:], key_scales[:])
+
+        gout_bf = interleave("gout_bf", gout_raw)
+        base_sb = sb.tile([P, I], F32, name="base_sb", tag="chain_b")
+        nc.sync.dma_start(base_sb[:], base)
+        val_scales = gather("val_scales", val_scale_pool, U8, "val_scales")
+        shift2 = placed.tile([P, 1], F32, name="shift2", offset=T // 2, align_bytes=MX_ALIGN)
+        gout_codes = placed.tile([P, Q], U32, name="gout_codes", offset=0, align_bytes=MX_ALIGN)
+        gout_mx = quantize("gout_scales", gout_bf, gout_codes)
+
+        minus_2a = row("minus_2a")
+        nc.vector.tensor_scalar(minus_2a[:], a[:], -2.0, None, ALU.mult, ALU.min, accum_out=shift2[:])
+
+        val_words = sb.tile([P, I], U16, name="val_words", tag="chain_c", align_bytes=MX_ALIGN)
+        c0 = []
+        for h, half in enumerate(HALVES):
+            entries = offsets[:, half.start // LIST_ROWS : half.stop // LIST_ROWS]
+            nc.vector.tensor_copy(val_words[:, half], val_pool[:].indirect(entries))
+            c0.append(product("c0_%d" % h, gout_mx, val_words[:, half], val_scales[:, half]))
 
         p, q, qq = row("p"), row("q"), row("qq")
-        s2, q2 = col("s2"), col("q2")
+        sum_q, sum_qq = col("sum_q"), col("sum_qq")
         shifts = col("shifts", 2)
-        nc.scalar.activation(shifts[:], powers[:], ACT.Copy, scale=neg_max[:])
-        nc.scalar.activation(q[:], a[:], ACT.Exp, scale=2.0, bias=neg_max[:], accum_out=s2[:])
-        nc.scalar.activation(p[:], a[:], ACT.Exp, bias=shifts[:, 0:1])
-        nc.scalar.activation(qq[:], a[:], ACT.Exp, scale=4.0, bias=shifts[:, 1:2], accum_out=q2[:])
+        nc.scalar.activation(shifts[:], max_factors[:], ACT.Copy, scale=shift2[:])
+        nc.scalar.activation(q[:], minus_2a[:], ACT.Exp, scale=-1.0, bias=shift2[:], accum_out=sum_q[:])
+        nc.scalar.activation(p[:], minus_2a[:], ACT.Exp, scale=-0.5, bias=shifts[:, 0:1])
+        nc.scalar.activation(qq[:], minus_2a[:], ACT.Exp, scale=-2.0, bias=shifts[:, 1:2], accum_out=sum_qq[:])
 
-        r = sb.tile([P, 1], F32, name="r", tag="words", align_bytes=64)
-        rv = col("rv", 4)
-        nq = sb.tile([P, 2], F32, name="nq", tag="picked", align_bytes=64)
-        nc.vector.reciprocal(r[:], s2[:])
-        nc.vector.tensor_scalar(rv[:, 0:3], factors[:], r[:], None, ALU.mult)
-        nc.vector.tensor_scalar(rv[:, 3:4], r[:], r[:], 5.0, ALU.mult, ALU.mult)
+        r = sb.tile([P, 1], F32, name="r", tag="chain_a", align_bytes=MX_ALIGN)
+        of_r = col("of_r", 4)
+        minus_r, half_r, mu_factors = of_r[:, 0:1], of_r[:, 2:3], of_r[:, 1:4]
+        qq_terms = sb.tile([P, 2], F32, name="qq_terms", tag="chain_c", align_bytes=MX_ALIGN)
+        nc.vector.reciprocal(r[:], sum_q[:])
+        nc.vector.tensor_scalar(of_r[:, 0:3], r_factors[:], r[:], None, ALU.mult)
+        nc.vector.tensor_scalar(of_r[:, 3:4], r[:], r[:], 5.0, ALU.mult, ALU.mult)
 
         u, uq, uu = row("u"), row("uq"), row("uu")
-        c_lo, c_hi, uq_lo, uq_hi, u2r = col("c_lo"), col("c_hi"), col("uq_lo"), col("uq_hi"), col("u2r")
-        mv_lo, mv = col("mv_lo", 3), col("mv", 3)
-        k3, bt_lo, bt, nb, k5 = col("k3"), col("bt_lo", 2), col("bt", 2), col("nb"), col("k5")
-        vn, b1, y, f1, x, res = row("vn"), row("b1"), row("y"), row("f1"), row("x"), row("res")
+        sum_u_lo, sum_u_hi = col("sum_u_lo"), col("sum_u_hi")
+        sum_uq_lo, sum_uq_hi = col("sum_uq_lo"), col("sum_uq_hi")
+        sum_uu = col("sum_uu")
+        of_mu_lo, of_mu = col("of_mu_lo", 3), col("of_mu", 3)
+        mu_15, mu_05, mu_5r = of_mu[:, 0:1], of_mu[:, 1:2], of_mu[:, 2:3]
+        brackets_lo, brackets = col("brackets_lo", 2), col("brackets", 2)
+        b = brackets[:, 0:1]
+        k2, k1, k0 = col("k2"), col("k1"), col("k0")
+        v, square, linear = row("v"), row("square"), row("linear")
+        base_qq, most, result = row("base_qq"), row("most"), row("result")
         root = math.sqrt(PENALTY)
-        nc.vector.scalar_tensor_tensor(u[:, lo], c[0][:], root, p[:, lo], ALU.mult, ALU.mult, accum_out=c_lo[:])
-        nc.vector.tensor_scalar(mv_lo[:], rv[:, 1:4], c_lo[:], None, ALU.mult)
-        nc.vector.scalar_tensor_tensor(u[:, hi], c[1][:], root, p[:, hi], ALU.mult, ALU.mult, accum_out=c_hi[:])
-        nc.vector.scalar_tensor_tensor(uq[:, lo], u[:, lo], rv[:, 2:3], q[:, lo], ALU.mult, ALU.mult, accum_out=uq_lo[:])
-        nc.vector.scalar_tensor_tensor(mv[:], rv[:, 1:4], c_hi[:], mv_lo[:], ALU.mult, ALU.add)
-        nc.vector.tensor_scalar(nq[:, 0:1], q2[:], r[:], -1.0 / 3.0, ALU.mult, ALU.mult)
-        nc.vector.tensor_scalar(nq[:, 1:2], q2[:], r[:], -1.0 / 5.0, ALU.mult, ALU.mult)
-        nc.vector.scalar_tensor_tensor(uq[:, hi], u[:, hi], rv[:, 2:3], q[:, hi], ALU.mult, ALU.mult, accum_out=uq_hi[:])
-        nc.scalar.activation(uu[:], u[:], ACT.Square, scale=r[:], accum_out=u2r[:])
-        nc.vector.tensor_scalar(bt_lo[:], nq[:], mv[:, 0:1], uq_lo[:], ALU.mult, ALU.add)
-        nc.vector.tensor_scalar(k3[:], mv[:, 1:2], mv[:, 1:2], rv[:, 0:1], ALU.mult, ALU.mult)
-        nc.vector.scalar_tensor_tensor(vn[:, lo], q[:, lo], mv[:, 0:1], u[:, lo], ALU.mult, ALU.subtract)
-        nc.vector.tensor_scalar(bt[:], bt_lo[:], uq_hi[:], None, ALU.add)
-        nc.vector.scalar_tensor_tensor(vn[:, hi], q[:, hi], mv[:, 0:1], u[:, hi], ALU.mult, ALU.subtract)
-        nc.vector.tensor_scalar(nb[:], bt[:, 0:1], bt[:, 0:1], rv[:, 0:1], ALU.mult, ALU.mult)
-        nc.vector.tensor_scalar(k5[:], bt[:, 1:2], mv[:, 2:3], u2r[:], ALU.mult, ALU.subtract)
-        for half in (lo, hi):
-            nc.vector.scalar_tensor_tensor(b1[:, half], qq[:, half], k3[:], base_sb[:, half], ALU.mult, ALU.add)
-        for half in (lo, hi):
-            nc.scalar.activation(f1[:, half], vn[:, half], ACT.Square, bias=bt[:, 0:1])
-        for half in (lo, hi):
-            nc.scalar.activation(y[:, half], q[:, half], ACT.Identity, scale=k5[:], bias=nb[:])
-        for half in (lo, hi):
-            nc.vector.scalar_tensor_tensor(x[:, half], f1[:, half], r[:], b1[:, half], ALU.mult, ALU.add)
-        for half, queue in ((lo, nc.sync), (hi, nc.scalar)):
-            nc.vector.tensor_tensor(res[:, half], x[:, half], y[:, half], ALU.add)
-            queue.dma_start(out[:, half], res[:, half])
+        nc.vector.scalar_tensor_tensor(u[:, lo], c0[0][:], root, p[:, lo], ALU.mult, ALU.mult, accum_out=sum_u_lo[:])
+        nc.vector.tensor_scalar(of_mu_lo[:], mu_factors, sum_u_lo[:], None, ALU.mult)
+        nc.vector.scalar_tensor_tensor(u[:, hi], c0[1][:], root, p[:, hi], ALU.mult, ALU.mult, accum_out=sum_u_hi[:])
+        nc.vector.scalar_tensor_tensor(uq[:, lo], u[:, lo], half_r, q[:, lo], ALU.mult, ALU.mult, accum_out=sum_uq_lo[:])
+        nc.vector.scalar_tensor_tensor(of_mu[:], mu_factors, sum_u_hi[:], of_mu_lo[:], ALU.mult, ALU.add)
+        nc.vector.tensor_scalar(qq_terms[:], fractions[:], sum_qq[:], r[:], ALU.mult, ALU.mult)
+        nc.vector.scalar_tensor_tensor(uq[:, hi], u[:, hi], half_r, q[:, hi], ALU.mult, ALU.mult, accum_out=sum_uq_hi[:])
+        nc.scalar.activation(uu[:], u[:], ACT.Square, scale=r[:], accum_out=sum_uu[:])
+        nc.vector.tensor_scalar(brackets_lo[:], qq_terms[:], mu_15, sum_uq_lo[:], ALU.mult, ALU.add)
+        nc.vector.tensor_scalar(k2[:], mu_05, mu_05, minus_r, ALU.mult, ALU.mult)
+        nc.vector.scalar_tensor_tensor(v[:, lo], q[:, lo], mu_15, u[:, lo], ALU.mult, ALU.subtract)
+        nc.vector.tensor_scalar(brackets[:], brackets_lo[:], sum_uq_hi[:], None, ALU.add)
+        nc.vector.scalar_tensor_tensor(v[:, hi], q[:, hi], mu_15, u[:, hi], ALU.mult, ALU.subtract)
+        nc.vector.tensor_scalar(k0[:], b, b, minus_r, ALU.mult, ALU.mult)
+        nc.vector.tensor_scalar(k1[:], brackets[:, 1:2], mu_5r, sum_uu[:], ALU.mult, ALU.subtract)
+
+        for half in HALVES:
+            nc.vector.scalar_tensor_tensor(base_qq[:, half], qq[:, half], k2[:], base_sb[:, half], ALU.mult, ALU.add)
+        for half in HALVES:
+            nc.scalar.activation(square[:, half], v[:, half], ACT.Square, bias=b)
+        for half in HALVES:
+            nc.scalar.activation(linear[:, half], q[:, half], ACT.Identity, scale=k1[:], bias=k0[:])
+        for half in HALVES:
+            nc.vector.scalar_tensor_tensor(most[:, half], square[:, half], r[:], base_qq[:, half], ALU.mult, ALU.add)
+        for half, queue in zip(HALVES, (nc.sync, nc.scalar)):
+            nc.vector.tensor_tensor(result[:, half], most[:, half], linear[:, half], ALU.add)
+            queue.dma_start(out[:, half], result[:, half])

import math
from contextlib import ExitStack

import concourse.mybir as mybir

D, E, T, I, Q = 512, 512, 2048, 512, 128
FLOPS = 2 * Q * I * (D + E)

F32 = mybir.dt.float32
BF16 = mybir.dt.bfloat16
I32 = mybir.dt.int32
U32 = mybir.dt.uint32
U16 = mybir.dt.uint16
U8 = mybir.dt.uint8
FP8X4 = mybir.dt.float8_e4m3fn_x4
FP4X4 = mybir.dt.float4_e2m1fn_x4
ALU = mybir.AluOpType
ACT = mybir.ActivationFunctionType

P = 128
PACK = 4
QUADRANT = 32
SCALE_ROWS = 4
LIST_ROWS = 16
PENALTY = 16.0 * 2.0 * 16.0
HALF = I // 2
HALVES = (slice(0, HALF), slice(HALF, I))
MX_ALIGN = 64


def tile_attend_gpunitweights_kernel(tc, query, keys_words, keys_scales, gout, vals_words, vals_scales, base, offs, out):
    nc = tc.nc
    lo, hi = HALVES
    with ExitStack() as ctx:
        sb = ctx.enter_context(tc.tile_pool(name="sb", bufs=1))
        placed = ctx.enter_context(tc.tile_pool(name="placed", bufs=1))
        ps = ctx.enter_context(tc.psum_pool(name="ps", bufs=1))

        def col(name, width=1):
            return sb.tile([P, width], F32, name=name)

        def row(name):
            return sb.tile([P, I], F32, name=name)

        def gather(name, pool, dtype, tag):
            picked = sb.tile([P, I], dtype, name=name, tag=tag, align_bytes=MX_ALIGN)
            nc.vector.tensor_copy(picked[:], pool[:].indirect(offsets[:]))
            return picked

        def interleave(name, raw):
            grouped = sb.tile([P, Q, PACK], BF16, name=name, align_bytes=MX_ALIGN)
            nc.scalar.copy(grouped[:], raw[:].rearrange("p t q -> p q t"))
            return grouped

        def quantize(name, grouped, codes):
            scales = sb.tile([P, Q], U8, name=name, align_bytes=MX_ALIGN)
            nc.vector.quantize_mx(
                out=codes[:].bitcast(FP8X4), scales=scales[:], in_=grouped[:].rearrange("p q t -> p (q t)")
            )
            return codes, scales

        def product(name, rows, words, scales):
            acc = ps.tile([P, words.shape[1]], F32, name=name)
            nc.tensor.matmul_mx(
                out=acc[:],
                lhsT=rows[0][:].bitcast(FP8X4),
                lhsT_scale=rows[1][:],
                rhs=words.bitcast(FP4X4),
                rhs_scale=scales,
                start=True,
                stop=True,
            )
            return acc

        offsets = sb.tile([P, I // LIST_ROWS], U16, name="offsets")
        key_pool = sb.tile([P, T], U16, name="key_pool", align_bytes=MX_ALIGN)
        key_scale_pool = sb.tile([P, T], U8, name="key_scale_pool", align_bytes=MX_ALIGN)
        val_scale_pool = placed.tile([P, T], U8, name="val_scale_pool", offset=0, align_bytes=MX_ALIGN)
        query_raw = sb.tile([P, PACK, Q], F32, name="query_raw", tag="chain_a", align_bytes=MX_ALIGN)

        nc.sync.dma_start(key_pool[:].bitcast(I32), keys_words[0].bitcast(I32))
        nc.sync.dma_start(offsets[:], offs)
        nc.sync.dma_start(query_raw[:], query.rearrange("(p t) q -> p t q", t=PACK))

        for pool, scales in ((key_scale_pool, keys_scales), (val_scale_pool, vals_scales)):
            nc.vector.memset(pool[:].bitcast(I32), 0)
            by_place = scales[0].rearrange("(g j) t -> j g t", j=SCALE_ROWS)
            for j in range(SCALE_ROWS):
                nc.sync.dma_start(pool[j:P:QUADRANT, :].bitcast(I32), by_place[j].bitcast(I32))

        zero = sb.tile([P, 1], F32, name="zero", tag="chain_b")
        one = col("one")
        fractions = col("fractions", 2)
        nc.vector.memset(zero[:], 0.0)
        nc.scalar.activation(one[:], zero[:], ACT.Exp)
        for j, value in enumerate((-1.0 / 3.0, -1.0 / 5.0)):
            nc.gpsimd.tensor_scalar(fractions[:, j : j + 1], one[:], value, 0.0, ALU.mult, ALU.add)
        gout_raw = sb.tile([P, PACK, Q], F32, name="gout_raw", tag="chain_b")
        nc.scalar.dma_start(gout_raw[:], gout.rearrange("(p t) q -> p t q", t=PACK))
        r_factors = col("r_factors", 3)
        for j, value in enumerate((-1.0, 1.5, 0.5)):
            nc.gpsimd.memset(r_factors[:, j : j + 1], value)
        max_factors = col("max_factors", 2)
        for j, value in enumerate((0.5, 2.0)):
            nc.gpsimd.memset(max_factors[:, j : j + 1], value)

        query_bf = interleave("query_bf", query_raw)
        key_words = gather("key_words", key_pool, U16, "chain_c")
        val_pool = sb.tile([P, T], U16, name="val_pool", tag="chain_a", align_bytes=MX_ALIGN)
        nc.sync.dma_start(val_pool[:].bitcast(I32), vals_words[0].bitcast(I32))
        key_scales = gather("key_scales", key_scale_pool, U8, "key_scales")
        query_codes = sb.tile([P, Q], U32, name="query_codes", align_bytes=MX_ALIGN)
        query_mx = quantize("query_scales", query_bf, query_codes)
        a = product("a", query_mx, key_words[:], key_scales[:])

        gout_bf = interleave("gout_bf", gout_raw)
        base_sb = sb.tile([P, I], F32, name="base_sb", tag="chain_b")
        nc.sync.dma_start(base_sb[:], base)
        val_scales = gather("val_scales", val_scale_pool, U8, "val_scales")
        shift2 = placed.tile([P, 1], F32, name="shift2", offset=T // 2, align_bytes=MX_ALIGN)
        gout_codes = placed.tile([P, Q], U32, name="gout_codes", offset=0, align_bytes=MX_ALIGN)
        gout_mx = quantize("gout_scales", gout_bf, gout_codes)

        minus_2a = row("minus_2a")
        nc.vector.tensor_scalar(minus_2a[:], a[:], -2.0, None, ALU.mult, ALU.min, accum_out=shift2[:])

        val_words = sb.tile([P, I], U16, name="val_words", tag="chain_c", align_bytes=MX_ALIGN)
        c0 = []
        for h, half in enumerate(HALVES):
            entries = offsets[:, half.start // LIST_ROWS : half.stop // LIST_ROWS]
            nc.vector.tensor_copy(val_words[:, half], val_pool[:].indirect(entries))
            c0.append(product("c0_%d" % h, gout_mx, val_words[:, half], val_scales[:, half]))

        p, q, qq = row("p"), row("q"), row("qq")
        sum_q, sum_qq = col("sum_q"), col("sum_qq")
        shifts = col("shifts", 2)
        nc.scalar.activation(shifts[:], max_factors[:], ACT.Copy, scale=shift2[:])
        nc.scalar.activation(q[:], minus_2a[:], ACT.Exp, scale=-1.0, bias=shift2[:], accum_out=sum_q[:])
        nc.scalar.activation(p[:], minus_2a[:], ACT.Exp, scale=-0.5, bias=shifts[:, 0:1])
        nc.scalar.activation(qq[:], minus_2a[:], ACT.Exp, scale=-2.0, bias=shifts[:, 1:2], accum_out=sum_qq[:])

        r = sb.tile([P, 1], F32, name="r", tag="chain_a", align_bytes=MX_ALIGN)
        of_r = col("of_r", 4)
        minus_r, half_r, mu_factors = of_r[:, 0:1], of_r[:, 2:3], of_r[:, 1:4]
        qq_terms = sb.tile([P, 2], F32, name="qq_terms", tag="chain_c", align_bytes=MX_ALIGN)
        nc.vector.reciprocal(r[:], sum_q[:])
        nc.vector.tensor_scalar(of_r[:, 0:3], r_factors[:], r[:], None, ALU.mult)
        nc.vector.tensor_scalar(of_r[:, 3:4], r[:], r[:], 5.0, ALU.mult, ALU.mult)

        u, uq, uu = row("u"), row("uq"), row("uu")
        sum_u_lo, sum_u_hi = col("sum_u_lo"), col("sum_u_hi")
        sum_uq_lo, sum_uq_hi = col("sum_uq_lo"), col("sum_uq_hi")
        sum_uu = col("sum_uu")
        of_mu_lo, of_mu = col("of_mu_lo", 3), col("of_mu", 3)
        mu_15, mu_05, mu_5r = of_mu[:, 0:1], of_mu[:, 1:2], of_mu[:, 2:3]
        brackets_lo, brackets = col("brackets_lo", 2), col("brackets", 2)
        b = brackets[:, 0:1]
        k2, k1, k0 = col("k2"), col("k1"), col("k0")
        v, square, linear = row("v"), row("square"), row("linear")
        base_qq, most, result = row("base_qq"), row("most"), row("result")
        root = math.sqrt(PENALTY)
        nc.vector.scalar_tensor_tensor(u[:, lo], c0[0][:], root, p[:, lo], ALU.mult, ALU.mult, accum_out=sum_u_lo[:])
        nc.vector.tensor_scalar(of_mu_lo[:], mu_factors, sum_u_lo[:], None, ALU.mult)
        nc.vector.scalar_tensor_tensor(u[:, hi], c0[1][:], root, p[:, hi], ALU.mult, ALU.mult, accum_out=sum_u_hi[:])
        nc.vector.scalar_tensor_tensor(uq[:, lo], u[:, lo], half_r, q[:, lo], ALU.mult, ALU.mult, accum_out=sum_uq_lo[:])
        nc.vector.scalar_tensor_tensor(of_mu[:], mu_factors, sum_u_hi[:], of_mu_lo[:], ALU.mult, ALU.add)
        nc.vector.tensor_scalar(qq_terms[:], fractions[:], sum_qq[:], r[:], ALU.mult, ALU.mult)
        nc.vector.scalar_tensor_tensor(uq[:, hi], u[:, hi], half_r, q[:, hi], ALU.mult, ALU.mult, accum_out=sum_uq_hi[:])
        nc.scalar.activation(uu[:], u[:], ACT.Square, scale=r[:], accum_out=sum_uu[:])
        nc.vector.tensor_scalar(brackets_lo[:], qq_terms[:], mu_15, sum_uq_lo[:], ALU.mult, ALU.add)
        nc.vector.tensor_scalar(k2[:], mu_05, mu_05, minus_r, ALU.mult, ALU.mult)
        nc.vector.scalar_tensor_tensor(v[:, lo], q[:, lo], mu_15, u[:, lo], ALU.mult, ALU.subtract)
        nc.vector.tensor_scalar(brackets[:], brackets_lo[:], sum_uq_hi[:], None, ALU.add)
        nc.vector.scalar_tensor_tensor(v[:, hi], q[:, hi], mu_15, u[:, hi], ALU.mult, ALU.subtract)
        nc.vector.tensor_scalar(k0[:], b, b, minus_r, ALU.mult, ALU.mult)
        nc.vector.tensor_scalar(k1[:], brackets[:, 1:2], mu_5r, sum_uu[:], ALU.mult, ALU.subtract)

        for half in HALVES:
            nc.vector.scalar_tensor_tensor(base_qq[:, half], qq[:, half], k2[:], base_sb[:, half], ALU.mult, ALU.add)
        for half in HALVES:
            nc.scalar.activation(square[:, half], v[:, half], ACT.Square, bias=b)
        for half in HALVES:
            nc.scalar.activation(linear[:, half], q[:, half], ACT.Identity, scale=k1[:], bias=k0[:])
        for half in HALVES:
            nc.vector.scalar_tensor_tensor(most[:, half], square[:, half], r[:], base_qq[:, half], ALU.mult, ALU.add)
        for half, queue in zip(HALVES, (nc.sync, nc.scalar)):
            nc.vector.tensor_tensor(result[:, half], most[:, half], linear[:, half], ALU.add)
            queue.dma_start(out[:, half], result[:, half])
